import numpy as np
import ml_dtypes


def mxq(x, axis, fmt="e4m3"):
    dtype, down = {"e4m3": (ml_dtypes.float8_e4m3fn, 7), "e5m2": (ml_dtypes.float8_e5m2, 14)}[fmt]
    v = np.moveaxis(np.asarray(x, np.float32).astype(ml_dtypes.bfloat16).astype(np.float64), axis, -1)
    blocks = v.reshape(v.shape[:-1] + (-1, 32))
    amax = np.abs(blocks).max(-1, keepdims=True)
    byte = np.maximum(np.where(amax > 0, np.frexp(amax)[1] - 1 + 127, 0) - down, 1)
    scale = np.exp2(byte - 127.0)
    codes = (blocks / scale).astype(np.float32).astype(dtype).astype(np.float64)
    return np.moveaxis((codes * scale).reshape(v.shape), -1, axis)


WIDE = False


def mx_kscale(k):
    if not WIDE:
        return np.ones(k)
    levels = np.array([10, -10, 5, -5, 0])
    if k % 512:
        return np.exp2(np.random.permutation(np.resize(levels, k // 32))).repeat(32)
    a = np.empty((k // 512, 16))
    for p in range(k // 512):
        a[p, :8] = np.random.permutation(np.resize(levels, 8))
        for g in range(8):
            far = levels[np.abs(levels - a[p, g]) >= 10]
            a[p, g + 8] = far[np.random.randint(len(far))]
    return np.exp2(a.ravel()).repeat(32)


def f64(x):
    return np.asarray(x).astype(np.float64)


def striped(idx):
    return np.tile(idx.reshape(-1, 16).T, (8, 1)).astype(np.uint16)


def unstriped(offs):
    return offs[:16].T.reshape(-1).astype(np.int64)


def pack_weight(w):
    k, n = w.shape
    w = f64(np.asarray(w, np.float32).astype(ml_dtypes.bfloat16)).reshape(k // 32, 32, n)
    amax = np.abs(w).max(1)
    byte = np.clip(np.where(amax > 0, np.frexp(amax)[1] - 1 + 127 - 7, 1), 1, 254)
    scaled = (w * np.exp2(127.0 - byte)[:, None, :]).reshape(k, n).astype(np.float32)
    words = np.ascontiguousarray(scaled.reshape(k // 512, 128, 4, n).transpose(0, 1, 3, 2)).astype(ml_dtypes.float8_e4m3fn).view(np.uint8)
    return words, np.ascontiguousarray(byte.astype(np.uint8).reshape(k // 512, 16, n))


def unpack_weight(words, scales):
    g, p, n, _ = words.shape
    vals = np.ascontiguousarray(words).view(ml_dtypes.float8_e4m3fn).astype(np.float64) * np.repeat(np.exp2(scales.astype(np.float64) - 127.0), 8, axis=1)[..., None]
    return vals.transpose(0, 1, 3, 2).reshape(g * 512, n)


K, T, S, H, C = 512, 2048, 256, 512, 512


def setup_inputs():
    n = np.random.standard_normal
    s = mx_kscale(K)[:, None]
    packed_xT = pack_weight(n((K, T)) * s)
    return {
        "x_words": packed_xT[0],
        "x_scales": packed_xT[1],
        "w1": (n((K, H)) / np.sqrt(K) / s).astype(np.float32),
        "gs": (np.random.uniform(0.5, 1.5, (K, 1)) / s).astype(np.float32),
        "offs": striped(np.random.permutation(T)[:S]),
        "n1": striped(np.random.permutation(S)),
        "n2": striped(np.random.permutation(S)),
        "ca": striped(np.random.permutation(T)[:C]),
        "cb": striped(np.random.permutation(T)[:C]),
        "n3": striped(np.random.permutation(S)),
        "n4": striped(np.random.permutation(S)),
        "n5": striped(np.random.permutation(S)),
        "n6": striped(np.random.permutation(S)),
    }


def reference(x_words, x_scales, w1, gs, offs, n1, n2, ca, cb, n3, n4, n5, n6):
    x_ca = unpack_weight(x_words, x_scales)[:, unstriped(ca)]
    xq = unpack_weight(x_words, x_scales)[:, unstriped(offs)]
    y = mxq(f64(w1), 0, "e4m3").T @ xq
    st = np.maximum(y, y[:, unstriped(n1)])
    z = f64(gs) * (st[:, unstriped(n2)] - (0.5 * y))
    zq = mxq(z, 0, "e4m3")
    a = 0.0625 * (x_ca.T @ zq)
    x_cb = unpack_weight(x_words, x_scales)[:, unstriped(cb)]
    b = 0.0625 * (x_cb.T @ zq)
    return np.maximum(a[:, unstriped(n3)] + b[:, unstriped(n5)], a[:, unstriped(n4)] + b[:, unstriped(n6)])

@@ -1,0 +1,146 @@
+from contextlib import ExitStack
+
+import concourse.mybir as mybir
+
+K, T, S, H, C = 512, 2048, 256, 512, 512
+FLOPS = 2 * K * S * (H + 2 * C)
+
+F32 = mybir.dt.float32
+BF16 = mybir.dt.bfloat16
+I32 = mybir.dt.int32
+U32 = mybir.dt.uint32
+U16 = mybir.dt.uint16
+U8 = mybir.dt.uint8
+FP8X4 = mybir.dt.float8_e4m3fn_x4
+ALU = mybir.AluOpType
+COPY = mybir.ActivationFunctionType.Copy
+
+P = 128
+PACK = 4
+SPARE = 8
+HALF = 256
+
+
+def tile_picked_ccmppathbhopb_none_p_kernel(tc, x_words, x_scales, w1, gs, offs, n1, n2, ca, cb, n3, n4, n5, n6, out):
+    nc = tc.nc
+    with ExitStack() as ctx:
+        keep = ctx.enter_context(tc.tile_pool(name="keep", bufs=1))
+        psum = ctx.enter_context(tc.psum_pool(name="psum", bufs=1))
+
+        def load_list(name, src):
+            lst = keep.tile(list(src.shape), U16, name=name)
+            nc.sync.dma_start(lst[:], src)
+            return lst
+
+        def window(name):
+            win = keep.tile([P, S + SPARE], F32, name=name)
+            nc.gpsimd.memset(win[:, S:], 0.0)
+            return win
+
+        xs = keep.tile([P, T], U8, align_bytes=64)
+        nc.vector.memset(xs[:].bitcast(I32), 0)
+        offs_t = load_list("offs_t", offs)
+        ca_t = load_list("ca_t", ca)
+        cb_t = load_list("cb_t", cb)
+        for q in range(4):
+            nc.sync.dma_start(xs[32 * q : 32 * q + 4, :].bitcast(I32), x_scales[0, 4 * q : 4 * q + 4, :].bitcast(I32))
+
+        w_raw = keep.tile([P, PACK, H], F32)
+        nc.sync.dma_start(w_raw[:], w1.rearrange("(p j) c -> p j c", j=PACK))
+        xw = keep.tile([P, T], U32, align_bytes=64)
+        nc.sync.dma_start(xw[:].bitcast(I32), x_words[0].rearrange("p n t -> p (n t)").bitcast(I32))
+        n1_t = load_list("n1_t", n1)
+        n2_t = load_list("n2_t", n2)
+        gs_t = keep.tile([P, PACK], F32)
+        nc.sync.dma_start(gs_t[:], gs.rearrange("(p t) o -> p (t o)", t=PACK))
+        n3_t = load_list("n3_t", n3)
+        n5_t = load_list("n5_t", n5)
+        n4_t = load_list("n4_t", n4)
+        n6_t = load_list("n6_t", n6)
+
+        def pick_bytes(name, lst, first, n):
+            picked = keep.tile([P, n], U8, name=name, align_bytes=64)
+            nc.vector.tensor_copy(picked[:], xs[:].indirect(lst[:, first // 16 : (first + n) // 16]))
+            return picked
+
+        def pick_words(name, lst, first, n):
+            picked = keep.tile([P, n], U32, name=name, align_bytes=64)
+            nc.vector.tensor_copy(picked[:], xw[:].indirect(lst[:, first // 16 : (first + n) // 16]))
+            return picked
+
+        xq_s = pick_bytes("xq_s", offs_t, 0, S)
+        ca_s = pick_bytes("ca_s", ca_t, 0, C)
+        cb_s = pick_bytes("cb_s", cb_t, 0, C)
+
+        w_codes = []
+        w_scales = []
+        for h in range(2):
+            w_bf = keep.tile([P, 2, P, PACK], BF16, align_bytes=64, name="w_bf%d" % h)
+            nc.scalar.copy(
+                w_bf[:].rearrange("p t m j -> p m t j"),
+                w_raw[:].rearrange("p j (m t) -> p m t j", t=PACK)[:, :, 2 * h : 2 * h + 2, :],
+            )
+            codes = keep.tile([P, 2 * P], U32, align_bytes=64, name="w_codes%d" % h)
+            scales = keep.tile([P, 2 * P], U8, align_bytes=64, name="w_scales%d" % h)
+            nc.vector.quantize_mx(out=codes[:].bitcast(FP8X4), scales=scales[:], in_=w_bf[:].rearrange("p t m j -> p (t m j)"))
+            w_codes.append(codes)
+            w_scales.append(scales)
+
+        xq_w = pick_words("xq_w", offs_t, 0, S)
+        ca_w = pick_words("ca_w", ca_t, 0, C)
+        cb_w = pick_words("cb_w", cb_t, 0, C)
+
+        us = []
+        for t in range(PACK):
+            cols = slice((t % 2) * P, (t % 2 + 1) * P)
+            y_ps = psum.tile([P, S], F32, name="y_ps", tag="bank%d" % t)
+            nc.tensor.matmul_mx(out=y_ps[:], lhsT=w_codes[t // 2][:, cols].bitcast(FP8X4), lhsT_scale=w_scales[t // 2][:, cols],
+                                rhs=xq_w[:].bitcast(FP8X4), rhs_scale=xq_s[:], start=True, stop=True)
+            yh = window("yh%d" % t)
+            nc.scalar.activation(yh[:, :S], y_ps[:], COPY, scale=-0.5)
+            g1 = keep.tile([P, S], F32, name="g1_%d" % t)
+            nc.scalar.activation(g1[:], yh[:].indirect(n1_t[:]), COPY)
+            st = window("st%d" % t)
+            nc.vector.scalar_tensor_tensor(st[:, :S], g1[:], -2.0, y_ps[:], ALU.mult, ALU.max)
+            u = keep.tile([P, S], F32, name="u%d" % t)
+            nc.vector.tensor_tensor(u[:], st[:].indirect(n2_t[:]), yh[:, :S], ALU.add)
+            us.append(u)
+
+        z_bf = keep.tile([P, S, PACK], BF16, align_bytes=64)
+        for t in range(PACK):
+            if t < 2:
+                nc.scalar.activation(z_bf[:, :, t], us[t][:], COPY, scale=gs_t[:, t : t + 1])
+            else:
+                nc.vector.tensor_scalar(z_bf[:, :, t], us[t][:], gs_t[:, t : t + 1], None, ALU.mult)
+        z_codes = keep.tile([P, S], U32, align_bytes=64)
+        z_scales = keep.tile([P, S], U8, align_bytes=64)
+        nc.vector.quantize_mx(out=z_codes[:].bitcast(FP8X4), scales=z_scales[:], in_=z_bf[:].rearrange("p n t -> p (n t)"))
+
+        for m in range(C // P):
+            wins = []
+            rows = slice(m * P, (m + 1) * P)
+            for i, (name, words, scales, bank) in enumerate((("a", ca_w, ca_s, 4 + m), ("b", cb_w, cb_s, m))):
+                ps = psum.tile([P, S], F32, name="ps", tag="bank%d" % bank)
+                nc.tensor.matmul_mx(out=ps[:], lhsT=words[:, rows].bitcast(FP8X4), lhsT_scale=scales[:, rows],
+                                    rhs=z_codes[:].bitcast(FP8X4), rhs_scale=z_scales[:], start=True, stop=True)
+                win = window("%s%d" % (name, m))
+                if i == 1:
+                    nc.vector.tensor_scalar(win[:, :S], ps[:], 0.0625, None, ALU.mult)
+                else:
+                    nc.scalar.activation(win[:, :S], ps[:], COPY, scale=0.0625)
+                wins.append(win)
+            sums = []
+            for k, (la, lb) in enumerate(((n3_t, n5_t), (n4_t, n6_t))):
+                ga = keep.tile([P, S], F32, name="ga%d_%d" % (m, k))
+                nc.scalar.activation(ga[:], wins[0][:].indirect(la[:]), COPY)
+                sm = keep.tile([P, S], F32, name="sm%d_%d" % (m, k))
+                if k == 1 and m % 2 == 1:
+                    gb = keep.tile([P, S], F32, name="gb%d_%d" % (m, k))
+                    nc.scalar.activation(gb[:], wins[1][:].indirect(lb[:]), COPY)
+                    nc.vector.tensor_tensor(sm[:], gb[:], ga[:], ALU.add)
+                else:
+                    nc.vector.tensor_tensor(sm[:], wins[1][:].indirect(lb[:]), ga[:], ALU.add)
+                sums.append(sm)
+            res = keep.tile([P, S], F32, name="res%d" % m)
+            nc.vector.tensor_tensor(res[:], sums[0][:], sums[1][:], ALU.max)
+            nc.sync.dma_start(out[m * P : (m + 1) * P, :], res[:])

@@ -34,11 +34,11 @@ def tile_picked_ccmppathbhopb_none_p_kernel(tc, x_words, x_scales, w1, gs, offs,
 
         def window(name):
             win = keep.tile([P, S + SPARE], F32, name=name)
-            nc.gpsimd.memset(win[:, S:], 0.0)
+            nc.vector.memset(win[:, S:], 0.0)
             return win
 
         xs = keep.tile([P, T], U8, align_bytes=64)
-        nc.vector.memset(xs[:].bitcast(I32), 0)
+        nc.gpsimd.memset(xs[:].bitcast(I32), 0)
         offs_t = load_list("offs_t", offs)
         ca_t = load_list("ca_t", ca)
         cb_t = load_list("cb_t", cb)
@@ -63,8 +63,8 @@ def tile_picked_ccmppathbhopb_none_p_kernel(tc, x_words, x_scales, w1, gs, offs,
             nc.vector.tensor_copy(picked[:], xs[:].indirect(lst[:, first // 16 : (first + n) // 16]))
             return picked
 
-        def pick_words(name, lst, first, n):
-            picked = keep.tile([P, n], U32, name=name, align_bytes=64)
+        def pick_words(name, lst, first, n, tag):
+            picked = keep.tile([P, n], U32, name=name, align_bytes=64, tag=tag)
             nc.vector.tensor_copy(picked[:], xw[:].indirect(lst[:, first // 16 : (first + n) // 16]))
             return picked
 
@@ -75,7 +75,7 @@ def tile_picked_ccmppathbhopb_none_p_kernel(tc, x_words, x_scales, w1, gs, offs,
         w_codes = []
         w_scales = []
         for h in range(2):
-            w_bf = keep.tile([P, 2, P, PACK], BF16, align_bytes=64, name="w_bf%d" % h)
+            w_bf = keep.tile([P, 2, P, PACK], BF16, align_bytes=64, name="w_bf", tag="stage%d" % h)
             nc.scalar.copy(
                 w_bf[:].rearrange("p t m j -> p m t j"),
                 w_raw[:].rearrange("p j (m t) -> p m t j", t=PACK)[:, :, 2 * h : 2 * h + 2, :],
@@ -86,9 +86,9 @@ def tile_picked_ccmppathbhopb_none_p_kernel(tc, x_words, x_scales, w1, gs, offs,
             w_codes.append(codes)
             w_scales.append(scales)
 
-        xq_w = pick_words("xq_w", offs_t, 0, S)
-        ca_w = pick_words("ca_w", ca_t, 0, C)
-        cb_w = pick_words("cb_w", cb_t, 0, C)
+        xq_w = pick_words("xq_w", offs_t, 0, S, "xq_w")
+        ca_w = pick_words("ca_w", ca_t, 0, C, "stage0")
+        cb_w = pick_words("cb_w", cb_t, 0, C, "stage1")
 
         us = []
         for t in range(PACK):
@@ -134,12 +134,7 @@ def tile_picked_ccmppathbhopb_none_p_kernel(tc, x_words, x_scales, w1, gs, offs,
                 ga = keep.tile([P, S], F32, name="ga%d_%d" % (m, k))
                 nc.scalar.activation(ga[:], wins[0][:].indirect(la[:]), COPY)
                 sm = keep.tile([P, S], F32, name="sm%d_%d" % (m, k))
-                if k == 1 and m % 2 == 1:
-                    gb = keep.tile([P, S], F32, name="gb%d_%d" % (m, k))
-                    nc.scalar.activation(gb[:], wins[1][:].indirect(lb[:]), COPY)
-                    nc.vector.tensor_tensor(sm[:], gb[:], ga[:], ALU.add)
-                else:
-                    nc.vector.tensor_tensor(sm[:], wins[1][:].indirect(lb[:]), ga[:], ALU.add)
+                nc.vector.tensor_tensor(sm[:], wins[1][:].indirect(lb[:]), ga[:], ALU.add)
                 sums.append(sm)
             res = keep.tile([P, S], F32, name="res%d" % m)
             nc.vector.tensor_tensor(res[:], sums[0][:], sums[1][:], ALU.max)

@@ -38,7 +38,8 @@ def tile_picked_ccmppathbhopb_none_p_kernel(tc, x_words, x_scales, w1, gs, offs,
             return win
 
         xs = keep.tile([P, T], U8, align_bytes=64)
-        nc.gpsimd.memset(xs[:].bitcast(I32), 0)
+        nc.gpsimd.memset(xs[:, : T // 2].bitcast(I32), 0)
+        nc.vector.memset(xs[:, T // 2 :].bitcast(I32), 0)
         offs_t = load_list("offs_t", offs)
         ca_t = load_list("ca_t", ca)
         cb_t = load_list("cb_t", cb)
@@ -88,7 +89,7 @@ def tile_picked_ccmppathbhopb_none_p_kernel(tc, x_words, x_scales, w1, gs, offs,
 
         xq_w = pick_words("xq_w", offs_t, 0, S, "xq_w")
         ca_w = pick_words("ca_w", ca_t, 0, C, "stage0")
-        cb_w = pick_words("cb_w", cb_t, 0, C, "stage1")
+        cb_w = [pick_words("cb_w0", cb_t, 0, HALF, "stage1")]
 
         us = []
         for t in range(PACK):
@@ -106,7 +107,7 @@ def tile_picked_ccmppathbhopb_none_p_kernel(tc, x_words, x_scales, w1, gs, offs,
             nc.vector.tensor_tensor(u[:], st[:].indirect(n2_t[:]), yh[:, :S], ALU.add)
             us.append(u)
 
-        z_bf = keep.tile([P, S, PACK], BF16, align_bytes=64)
+        z_bf = keep.tile([P, S, PACK], BF16, align_bytes=64, tag="stage2")
         for t in range(PACK):
             if t < 2:
                 nc.scalar.activation(z_bf[:, :, t], us[t][:], COPY, scale=gs_t[:, t : t + 1])
@@ -116,26 +117,42 @@ def tile_picked_ccmppathbhopb_none_p_kernel(tc, x_words, x_scales, w1, gs, offs,
         z_scales = keep.tile([P, S], U8, align_bytes=64)
         nc.vector.quantize_mx(out=z_codes[:].bitcast(FP8X4), scales=z_scales[:], in_=z_bf[:].rearrange("p n t -> p (n t)"))
 
-        for m in range(C // P):
-            wins = []
+        cb_w.append(pick_words("cb_w1", cb_t, HALF, HALF, "stage2"))
+
+        blocks = C // P
+        for m in range(blocks):
             rows = slice(m * P, (m + 1) * P)
-            for i, (name, words, scales, bank) in enumerate((("a", ca_w, ca_s, 4 + m), ("b", cb_w, cb_s, m))):
-                ps = psum.tile([P, S], F32, name="ps", tag="bank%d" % bank)
-                nc.tensor.matmul_mx(out=ps[:], lhsT=words[:, rows].bitcast(FP8X4), lhsT_scale=scales[:, rows],
-                                    rhs=z_codes[:].bitcast(FP8X4), rhs_scale=z_scales[:], start=True, stop=True)
-                win = window("%s%d" % (name, m))
-                if i == 1:
-                    nc.vector.tensor_scalar(win[:, :S], ps[:], 0.0625, None, ALU.mult)
+            a_ps = psum.tile([P, S], F32, name="a_ps", tag="bank%d" % (PACK + m))
+            nc.tensor.matmul_mx(out=a_ps[:], lhsT=ca_w[:, rows].bitcast(FP8X4), lhsT_scale=ca_s[:, rows],
+                                rhs=z_codes[:].bitcast(FP8X4), rhs_scale=z_scales[:], start=True, stop=True)
+            b_ps = psum.tile([P, S], F32, name="b_ps", tag="bank%d" % m)
+            nc.tensor.matmul_mx(out=b_ps[:], lhsT=cb_w[m // 2][:, (m % 2) * P : (m % 2 + 1) * P].bitcast(FP8X4), lhsT_scale=cb_s[:, rows],
+                                rhs=z_codes[:].bitcast(FP8X4), rhs_scale=z_scales[:], start=True, stop=True)
+            a_win = window("a%d" % m)
+            nc.scalar.activation(a_win[:, :S], a_ps[:], COPY, scale=0.0625)
+            b_win = window("b%d" % m)
+            nc.vector.tensor_scalar(b_win[:, :S], b_ps[:], 0.0625, None, ALU.mult)
+
+            def fetch(name, win, lst, first, n):
+                got = keep.tile([P, n], F32, name=name)
+                nc.scalar.activation(got[:], win[:].indirect(lst[:, first // 16 : (first + n) // 16]), COPY)
+                return got
+
+            a3 = fetch("a3_%d" % m, a_win, n3_t, 0, S)
+            s1 = keep.tile([P, S], F32, name="s1_%d" % m)
+            nc.vector.tensor_tensor(s1[:], b_win[:].indirect(n5_t[:]), a3[:], ALU.add)
+            last = m == blocks - 1
+            if last:
+                b6 = fetch("b6", b_win, n6_t, 0, S)
+            n = S // 2 if last else S
+            for first in range(0, S, n):
+                cols = slice(first, first + n)
+                a4 = fetch("a4_%d_%d" % (m, first), a_win, n4_t, first, n)
+                s2 = keep.tile([P, n], F32, name="s2_%d_%d" % (m, first))
+                if last:
+                    nc.vector.tensor_tensor(s2[:], b6[:, cols], a4[:], ALU.add)
                 else:
-                    nc.scalar.activation(win[:, :S], ps[:], COPY, scale=0.0625)
-                wins.append(win)
-            sums = []
-            for k, (la, lb) in enumerate(((n3_t, n5_t), (n4_t, n6_t))):
-                ga = keep.tile([P, S], F32, name="ga%d_%d" % (m, k))
-                nc.scalar.activation(ga[:], wins[0][:].indirect(la[:]), COPY)
-                sm = keep.tile([P, S], F32, name="sm%d_%d" % (m, k))
-                nc.vector.tensor_tensor(sm[:], wins[1][:].indirect(lb[:]), ga[:], ALU.add)
-                sums.append(sm)
-            res = keep.tile([P, S], F32, name="res%d" % m)
-            nc.vector.tensor_tensor(res[:], sums[0][:], sums[1][:], ALU.max)
-            nc.sync.dma_start(out[m * P : (m + 1) * P, :], res[:])
+                    nc.vector.tensor_tensor(s2[:], b_win[:].indirect(n6_t[:]), a4[:], ALU.add)
+                res = keep.tile([P, n], F32, name="res%d_%d" % (m, first))
+                nc.vector.tensor_tensor(res[:], s1[:, cols], s2[:], ALU.max)
+                nc.sync.dma_start(out[rows, cols], res[:])

@@ -107,15 +107,20 @@ def tile_picked_ccmppathbhopb_none_p_kernel(tc, x_words, x_scales, w1, gs, offs,
             nc.vector.tensor_tensor(u[:], st[:].indirect(n2_t[:]), yh[:, :S], ALU.add)
             us.append(u)
 
+        halves = (slice(0, S // 2), slice(S // 2, S))
         z_bf = keep.tile([P, S, PACK], BF16, align_bytes=64, tag="stage2")
         for t in range(PACK):
             if t < 2:
                 nc.scalar.activation(z_bf[:, :, t], us[t][:], COPY, scale=gs_t[:, t : t + 1])
-            else:
+            elif t == 2:
                 nc.vector.tensor_scalar(z_bf[:, :, t], us[t][:], gs_t[:, t : t + 1], None, ALU.mult)
+            else:
+                for cols in halves:
+                    nc.vector.tensor_scalar(z_bf[:, cols, t], us[t][:, cols], gs_t[:, t : t + 1], None, ALU.mult)
         z_codes = keep.tile([P, S], U32, align_bytes=64)
         z_scales = keep.tile([P, S], U8, align_bytes=64)
-        nc.vector.quantize_mx(out=z_codes[:].bitcast(FP8X4), scales=z_scales[:], in_=z_bf[:].rearrange("p n t -> p (n t)"))
+        for cols in halves:
+            nc.vector.quantize_mx(out=z_codes[:, cols].bitcast(FP8X4), scales=z_scales[:, cols], in_=z_bf[:, cols, :].rearrange("p n t -> p (n t)"))
 
         cb_w.append(pick_words("cb_w1", cb_t, HALF, HALF, "stage2"))
 

from contextlib import ExitStack

import concourse.mybir as mybir

K, T, S, H, C = 512, 2048, 256, 512, 512
FLOPS = 2 * K * S * (H + 2 * C)

F32 = mybir.dt.float32
BF16 = mybir.dt.bfloat16
I32 = mybir.dt.int32
U32 = mybir.dt.uint32
U16 = mybir.dt.uint16
U8 = mybir.dt.uint8
FP8X4 = mybir.dt.float8_e4m3fn_x4
ALU = mybir.AluOpType
COPY = mybir.ActivationFunctionType.Copy

P = 128
PACK = 4
SPARE = 8
HALF = 256


def tile_picked_ccmppathbhopb_none_p_kernel(tc, x_words, x_scales, w1, gs, offs, n1, n2, ca, cb, n3, n4, n5, n6, out):
    nc = tc.nc
    with ExitStack() as ctx:
        keep = ctx.enter_context(tc.tile_pool(name="keep", bufs=1))
        psum = ctx.enter_context(tc.psum_pool(name="psum", bufs=1))

        def load_list(name, src):
            lst = keep.tile(list(src.shape), U16, name=name)
            nc.sync.dma_start(lst[:], src)
            return lst

        def window(name):
            win = keep.tile([P, S + SPARE], F32, name=name)
            nc.vector.memset(win[:, S:], 0.0)
            return win

        xs = keep.tile([P, T], U8, align_bytes=64)
        nc.gpsimd.memset(xs[:, : T // 2].bitcast(I32), 0)
        nc.vector.memset(xs[:, T // 2 :].bitcast(I32), 0)
        offs_t = load_list("offs_t", offs)
        ca_t = load_list("ca_t", ca)
        cb_t = load_list("cb_t", cb)
        for q in range(4):
            nc.sync.dma_start(xs[32 * q : 32 * q + 4, :].bitcast(I32), x_scales[0, 4 * q : 4 * q + 4, :].bitcast(I32))

        w_raw = keep.tile([P, PACK, H], F32)
        nc.sync.dma_start(w_raw[:], w1.rearrange("(p j) c -> p j c", j=PACK))
        xw = keep.tile([P, T], U32, align_bytes=64)
        nc.sync.dma_start(xw[:].bitcast(I32), x_words[0].rearrange("p n t -> p (n t)").bitcast(I32))
        n1_t = load_list("n1_t", n1)
        n2_t = load_list("n2_t", n2)
        gs_t = keep.tile([P, PACK], F32)
        nc.sync.dma_start(gs_t[:], gs.rearrange("(p t) o -> p (t o)", t=PACK))
        n3_t = load_list("n3_t", n3)
        n5_t = load_list("n5_t", n5)
        n4_t = load_list("n4_t", n4)
        n6_t = load_list("n6_t", n6)

        def pick_bytes(name, lst, first, n):
            picked = keep.tile([P, n], U8, name=name, align_bytes=64)
            nc.vector.tensor_copy(picked[:], xs[:].indirect(lst[:, first // 16 : (first + n) // 16]))
            return picked

        def pick_words(name, lst, first, n, tag):
            picked = keep.tile([P, n], U32, name=name, align_bytes=64, tag=tag)
            nc.vector.tensor_copy(picked[:], xw[:].indirect(lst[:, first // 16 : (first + n) // 16]))
            return picked

        xq_s = pick_bytes("xq_s", offs_t, 0, S)
        ca_s = pick_bytes("ca_s", ca_t, 0, C)
        cb_s = pick_bytes("cb_s", cb_t, 0, C)

        w_codes = []
        w_scales = []
        for h in range(2):
            w_bf = keep.tile([P, 2, P, PACK], BF16, align_bytes=64, name="w_bf", tag="stage%d" % h)
            nc.scalar.copy(
                w_bf[:].rearrange("p t m j -> p m t j"),
                w_raw[:].rearrange("p j (m t) -> p m t j", t=PACK)[:, :, 2 * h : 2 * h + 2, :],
            )
            codes = keep.tile([P, 2 * P], U32, align_bytes=64, name="w_codes%d" % h)
            scales = keep.tile([P, 2 * P], U8, align_bytes=64, name="w_scales%d" % h)
            nc.vector.quantize_mx(out=codes[:].bitcast(FP8X4), scales=scales[:], in_=w_bf[:].rearrange("p t m j -> p (t m j)"))
            w_codes.append(codes)
            w_scales.append(scales)

        xq_w = pick_words("xq_w", offs_t, 0, S, "xq_w")
        ca_w = pick_words("ca_w", ca_t, 0, C, "stage0")
        cb_w = [pick_words("cb_w0", cb_t, 0, HALF, "stage1")]

        us = []
        for t in range(PACK):
            cols = slice((t % 2) * P, (t % 2 + 1) * P)
            y_ps = psum.tile([P, S], F32, name="y_ps", tag="bank%d" % t)
            nc.tensor.matmul_mx(out=y_ps[:], lhsT=w_codes[t // 2][:, cols].bitcast(FP8X4), lhsT_scale=w_scales[t // 2][:, cols],
                                rhs=xq_w[:].bitcast(FP8X4), rhs_scale=xq_s[:], start=True, stop=True)
            yh = window("yh%d" % t)
            nc.scalar.activation(yh[:, :S], y_ps[:], COPY, scale=-0.5)
            g1 = keep.tile([P, S], F32, name="g1_%d" % t)
            nc.scalar.activation(g1[:], yh[:].indirect(n1_t[:]), COPY)
            st = window("st%d" % t)
            nc.vector.scalar_tensor_tensor(st[:, :S], g1[:], -2.0, y_ps[:], ALU.mult, ALU.max)
            u = keep.tile([P, S], F32, name="u%d" % t)
            nc.vector.tensor_tensor(u[:], st[:].indirect(n2_t[:]), yh[:, :S], ALU.add)
            us.append(u)

        halves = (slice(0, S // 2), slice(S // 2, S))
        z_bf = keep.tile([P, S, PACK], BF16, align_bytes=64, tag="stage2")
        for t in range(PACK):
            if t < 2:
                nc.scalar.activation(z_bf[:, :, t], us[t][:], COPY, scale=gs_t[:, t : t + 1])
            elif t == 2:
                nc.vector.tensor_scalar(z_bf[:, :, t], us[t][:], gs_t[:, t : t + 1], None, ALU.mult)
            else:
                for cols in halves:
                    nc.vector.tensor_scalar(z_bf[:, cols, t], us[t][:, cols], gs_t[:, t : t + 1], None, ALU.mult)
        z_codes = keep.tile([P, S], U32, align_bytes=64)
        z_scales = keep.tile([P, S], U8, align_bytes=64)
        for cols in halves:
            nc.vector.quantize_mx(out=z_codes[:, cols].bitcast(FP8X4), scales=z_scales[:, cols], in_=z_bf[:, cols, :].rearrange("p n t -> p (n t)"))

        cb_w.append(pick_words("cb_w1", cb_t, HALF, HALF, "stage2"))

        blocks = C // P
        for m in range(blocks):
            rows = slice(m * P, (m + 1) * P)
            a_ps = psum.tile([P, S], F32, name="a_ps", tag="bank%d" % (PACK + m))
            nc.tensor.matmul_mx(out=a_ps[:], lhsT=ca_w[:, rows].bitcast(FP8X4), lhsT_scale=ca_s[:, rows],
                                rhs=z_codes[:].bitcast(FP8X4), rhs_scale=z_scales[:], start=True, stop=True)
            b_ps = psum.tile([P, S], F32, name="b_ps", tag="bank%d" % m)
            nc.tensor.matmul_mx(out=b_ps[:], lhsT=cb_w[m // 2][:, (m % 2) * P : (m % 2 + 1) * P].bitcast(FP8X4), lhsT_scale=cb_s[:, rows],
                                rhs=z_codes[:].bitcast(FP8X4), rhs_scale=z_scales[:], start=True, stop=True)
            a_win = window("a%d" % m)
            nc.scalar.activation(a_win[:, :S], a_ps[:], COPY, scale=0.0625)
            b_win = window("b%d" % m)
            nc.vector.tensor_scalar(b_win[:, :S], b_ps[:], 0.0625, None, ALU.mult)

            def fetch(name, win, lst, first, n):
                got = keep.tile([P, n], F32, name=name)
                nc.scalar.activation(got[:], win[:].indirect(lst[:, first // 16 : (first + n) // 16]), COPY)
                return got

            a3 = fetch("a3_%d" % m, a_win, n3_t, 0, S)
            s1 = keep.tile([P, S], F32, name="s1_%d" % m)
            nc.vector.tensor_tensor(s1[:], b_win[:].indirect(n5_t[:]), a3[:], ALU.add)
            last = m == blocks - 1
            if last:
                b6 = fetch("b6", b_win, n6_t, 0, S)
            n = S // 2 if last else S
            for first in range(0, S, n):
                cols = slice(first, first + n)
                a4 = fetch("a4_%d_%d" % (m, first), a_win, n4_t, first, n)
                s2 = keep.tile([P, n], F32, name="s2_%d_%d" % (m, first))
                if last:
                    nc.vector.tensor_tensor(s2[:], b6[:, cols], a4[:], ALU.add)
                else:
                    nc.vector.tensor_tensor(s2[:], b_win[:].indirect(n6_t[:]), a4[:], ALU.add)
                res = keep.tile([P, n], F32, name="res%d_%d" % (m, first))
                nc.vector.tensor_tensor(res[:], s1[:, cols], s2[:], ALU.max)
                nc.sync.dma_start(out[rows, cols], res[:])
